import numpy as np
import ml_dtypes


def mxq(x, axis, fmt="e4m3"):
    dtype, down = {"e4m3": (ml_dtypes.float8_e4m3fn, 7), "e5m2": (ml_dtypes.float8_e5m2, 14)}[fmt]
    v = np.moveaxis(np.asarray(x, np.float32).astype(ml_dtypes.bfloat16).astype(np.float64), axis, -1)
    blocks = v.reshape(v.shape[:-1] + (-1, 32))
    amax = np.abs(blocks).max(-1, keepdims=True)
    byte = np.maximum(np.where(amax > 0, np.frexp(amax)[1] - 1 + 127, 0) - down, 1)
    scale = np.exp2(byte - 127.0)
    codes = (blocks / scale).astype(np.float32).astype(dtype).astype(np.float64)
    return np.moveaxis((codes * scale).reshape(v.shape), -1, axis)


WIDE = False


def mx_kscale(k):
    if not WIDE:
        return np.ones(k)
    levels = np.array([10, -10, 5, -5, 0])
    if k % 512:
        return np.exp2(np.random.permutation(np.resize(levels, k // 32))).repeat(32)
    a = np.empty((k // 512, 16))
    for p in range(k // 512):
        a[p, :8] = np.random.permutation(np.resize(levels, 8))
        for g in range(8):
            far = levels[np.abs(levels - a[p, g]) >= 10]
            a[p, g + 8] = far[np.random.randint(len(far))]
    return np.exp2(a.ravel()).repeat(32)


def f64(x):
    return np.asarray(x).astype(np.float64)


def striped8(idx):
    return np.asarray(idx).reshape(8, -1, 16).transpose(0, 2, 1).reshape(128, -1).astype(np.uint16)


def unstriped8(offs):
    return offs.reshape(8, 16, -1).transpose(0, 2, 1).reshape(8, -1).astype(np.int64)


def pick8(x, idx, run):
    r = np.arange(len(x))
    return x[r[:, None], idx[r % (8 * run) // run]]


E2M1 = np.array([0.0, 0.5, 1.0, 1.5, 2.0, 3.0, 4.0, 6.0, -0.0, -0.5, -1.0, -1.5, -2.0, -3.0, -4.0, -6.0])


def pack_weight(w, fmt):
    k, n = w.shape
    w = f64(np.asarray(w, np.float32).astype(ml_dtypes.bfloat16)).reshape(k // 32, 32, n)
    amax = np.abs(w).max(1)
    if fmt == "e4m3":
        byte = np.frexp(amax)[1] - 1 + 127 - 7
    else:
        mant, ex = np.frexp(amax / 6.0)
        byte = np.where(mant > 0.5, ex, ex - 1) + 127
    byte = np.clip(np.where(amax > 0, byte, 1), 1, 254)
    scaled = (w * np.exp2(127.0 - byte)[:, None, :]).reshape(k, n).astype(np.float32)
    by_word = np.ascontiguousarray(scaled.reshape(k // 512, 128, 4, n).transpose(0, 1, 3, 2))
    if fmt == "e4m3":
        words = by_word.astype(ml_dtypes.float8_e4m3fn).view(np.uint8)
    else:
        c = by_word.astype(ml_dtypes.float4_e2m1fn).view(np.uint8) & 0xF
        words = (c[..., 0::2] | (c[..., 1::2] << 4)).reshape(k // 512, 128, 2 * n)
    return np.ascontiguousarray(words), np.ascontiguousarray(byte.astype(np.uint8).reshape(k // 512, 16, n))


def unpack_weight(words, scales, fmt):
    g, _, n = scales.shape
    words = np.ascontiguousarray(words).reshape(g, 128, n, -1)
    if fmt == "e4m3":
        vals = words.view(ml_dtypes.float8_e4m3fn).astype(np.float64)
    else:
        nib = np.empty((g, 128, n, 4), np.uint8)
        nib[..., 0::2] = words & 0xF
        nib[..., 1::2] = words >> 4
        vals = E2M1[nib]
    vals = vals * np.repeat(np.exp2(scales.astype(np.float64) - 127.0), 8, axis=1)[..., None]
    return vals.transpose(0, 1, 3, 2).reshape(g * 512, n)


D, T, I, Q = 512, 1024, 512, 128


def setup_inputs():
    n = np.random.standard_normal
    idx = np.stack([np.random.permutation(T)[:I] for _ in range(8)])
    idx2 = np.stack([np.random.permutation(T)[:I] for _ in range(8)])
    idx3 = np.stack([np.random.permutation(T)[:I] for _ in range(8)])
    fd = mx_kscale(D)
    keysp = pack_weight(n((D, T)) / fd[:, None], "e4m3")
    return {
        "query": (n((D, Q)) * 0.9 / np.sqrt(D) * fd[:, None]).astype(np.float32),
        "query2": (n((D, Q)) * 0.9 / np.sqrt(D) * fd[:, None]).astype(np.float32),
        "keys_words": keysp[0],
        "keys_scales": keysp[1],
        "lam": (np.random.uniform(1.0, 2.5, (Q, 1))).astype(np.float32),
        "lean": (np.random.uniform(0.2, 0.6, (Q, 1))).astype(np.float32),
        "base": (0.3 * n((Q, I))).astype(np.float32),
        "gain2": (np.random.uniform(0.5, 2.0, (Q, 1))).astype(np.float32),
        "offs": striped8(idx),
        "offs2": striped8(idx2),
        "offs3": striped8(idx3),
    }


def reference(query, query2, keys_words, keys_scales, lam, lean, base, gain2, offs, offs2, offs3):
    idx = unstriped8(offs)
    idx2 = unstriped8(offs2)
    idx3 = unstriped8(offs3)
    keysu = unpack_weight(keys_words, keys_scales, "e4m3")
    queryq = mxq(f64(query), 0, "e4m3")
    a = queryq.T @ keysu
    query2q = mxq(f64(query2), 0, "e4m3")
    b = query2q.T @ keysu
    e1s = np.exp(pick8(a, idx, 16))
    s = e1s / (e1s + np.exp(pick8(a, idx2, 16)) + np.exp(pick8(b, idx3, 16))) * f64(lam)
    p = np.exp(s - np.max(s, axis=1, keepdims=True))
    r = p / np.sum(p, axis=1, keepdims=True)
    m0 = np.sum(r * s, axis=1, keepdims=True)
    w = r * ((s - m0) * f64(lean) + 1.0)
    y = np.tanh(w * f64(gain2) * 128.0) + f64(base)
    return y

@@ -1,0 +1,186 @@
+from contextlib import ExitStack
+
+import concourse.mybir as mybir
+
+D, T, I, Q = 512, 1024, 512, 128
+FLOPS = 2 * 2 * D * T * Q
+
+F32 = mybir.dt.float32
+BF16 = mybir.dt.bfloat16
+I32 = mybir.dt.int32
+U32 = mybir.dt.uint32
+U16 = mybir.dt.uint16
+U8 = mybir.dt.uint8
+FP8X4 = mybir.dt.float8_e4m3fn_x4
+ALU = mybir.AluOpType
+ACT = mybir.ActivationFunctionType
+
+P = 128
+PACK = 4
+HALVES = 2
+W = I // HALVES
+LIST_COLS = W // 16
+A_PIECE = 256
+KEY_PIECE = 512
+CAP = 20.0
+
+
+def tile_attend_quotaratio_leaning_gated_heads_kernel(
+    tc, query, query2, keys_words, keys_scales, lam, lean, base, gain2, offs, offs2, offs3, out
+):
+    nc = tc.nc
+    with ExitStack() as ctx:
+        keep = ctx.enter_context(tc.tile_pool(name="keep", bufs=1))
+        psum = ctx.enter_context(tc.psum_pool(name="psum", bufs=1))
+
+        def column(name):
+            return keep.tile([P, 1], F32, name=name)
+
+        def wide(name, shape):
+            return keep.tile([P] + shape, F32, name=name)
+
+        lam_sb, lean_sb, gain_sb = column("lam_sb"), column("lean_sb"), column("gain_sb")
+        key_scales = keep.tile([P, T], U8, name="key_scales", align_bytes=64)
+
+        raw = [wide("raw_q%d" % n, [PACK, Q]) for n in range(2)]
+        key_words = [
+            keep.tile([P, KEY_PIECE], U32, name="key_words%d" % n, align_bytes=64)
+            for n in range(T // KEY_PIECE)
+        ]
+        words_hbm = keys_words[0].rearrange("p n t -> p (n t)")
+        nc.sync.dma_start(out=raw[0][:], in_=query.rearrange("(p j) w -> p j w", j=PACK))
+        for r in range(4):
+            nc.scalar.dma_start(
+                out=key_scales[r:P:32, :].bitcast(I32), in_=keys_scales[0][r:16:4, :].bitcast(I32)
+            )
+        for n in range(T // KEY_PIECE):
+            piece = slice(n * KEY_PIECE * PACK, (n + 1) * KEY_PIECE * PACK)
+            nc.sync.dma_start(out=key_words[n][:].bitcast(I32), in_=words_hbm[:, piece].bitcast(I32))
+        nc.sync.dma_start(out=raw[1][:], in_=query2.rearrange("(p j) w -> p j w", j=PACK))
+        lists = []
+        for name, src in (("offs_sb", offs), ("offs2_sb", offs2), ("offs3_sb", offs3)):
+            tile = keep.tile([P, I // 16], U16, name=name)
+            nc.sync.dma_start(tile[:], src)
+            lists.append(tile)
+        base_sb = wide("base_sb", [I])
+        nc.sync.dma_start(out=base_sb[:], in_=base)
+        nc.gpsimd.dma_start(out=lam_sb[:], in_=lam)
+        nc.gpsimd.dma_start(out=lean_sb[:], in_=lean)
+        nc.gpsimd.dma_start(out=gain_sb[:], in_=gain2)
+
+        cap = column("cap")
+        nc.gpsimd.memset(cap[:], CAP)
+        lam_abs, lam_neg, lam_ge, lam_sign = (
+            column("lam_abs"), column("lam_neg"), column("lam_ge"), column("lam_sign"),
+        )
+        slope, gain128 = column("slope"), column("gain128")
+        nc.scalar.activation(out=lam_abs[:], in_=lam_sb[:], func=ACT.Abs)
+        nc.gpsimd.tensor_scalar(lam_ge[:], lam_sb[:], 0.0, None, ALU.is_ge)
+        nc.gpsimd.tensor_scalar(lam_sign[:], lam_ge[:], 2.0, -1.0, ALU.mult, ALU.add)
+        nc.gpsimd.tensor_scalar(lam_neg[:], lam_abs[:], -1.0, 0.0, ALU.mult, ALU.add)
+        nc.gpsimd.tensor_tensor(slope[:], lam_abs[:], lean_sb[:], ALU.mult)
+        nc.gpsimd.tensor_scalar(gain128[:], gain_sb[:], 128.0, 0.0, ALU.mult, ALU.add)
+
+        a_sb, b_sb = wide("a_sb", [T]), wide("b_sb", [T])
+        for n, (scores, piece) in enumerate(((a_sb, A_PIECE), (b_sb, KEY_PIECE))):
+            grouped = keep.tile([P, Q, PACK], BF16, name="grouped%d" % n, align_bytes=64)
+            codes = keep.tile([P, Q], U32, name="codes%d" % n, align_bytes=64)
+            scales = keep.tile([P, Q], U8, name="scales%d" % n, align_bytes=64)
+            nc.vector.tensor_copy(out=grouped[:], in_=raw[n][:].rearrange("p j w -> p w j"))
+            nc.vector.quantize_mx(
+                out=codes[:].bitcast(FP8X4), scales=scales[:], in_=grouped[:].rearrange("p w j -> p (w j)")
+            )
+            for c in range(T // piece):
+                t0 = c * piece
+                bank = psum.tile([P, piece], F32, name="bank%d_%d" % (n, c))
+                within = slice(t0 % KEY_PIECE, t0 % KEY_PIECE + piece)
+                nc.tensor.matmul_mx(
+                    out=bank[:],
+                    lhsT=codes[:].bitcast(FP8X4),
+                    lhsT_scale=scales[:],
+                    rhs=key_words[t0 // KEY_PIECE][:, within].bitcast(FP8X4),
+                    rhs_scale=key_scales[:, t0 : t0 + piece],
+                    start=True,
+                    stop=True,
+                )
+                on_scalar = c % 2 == n
+                if on_scalar:
+                    nc.scalar.copy(out=scores[:, t0 : t0 + piece], in_=bank[:])
+                else:
+                    nc.vector.tensor_copy(out=scores[:, t0 : t0 + piece], in_=bank[:])
+
+        signed, lowest = [], []
+        for h in range(HALVES):
+            cols = slice(h * LIST_COLS, (h + 1) * LIST_COLS)
+            first = wide("first%d" % h, [W])
+            nc.scalar.activation(out=first[:], in_=a_sb[:].indirect(lists[0][:, cols]), func=ACT.Copy)
+            powers = []
+            for j, (table, listed) in enumerate(((a_sb, lists[1]), (b_sb, lists[2]))):
+                diff, room, power = (
+                    wide("diff%d_%d" % (h, j), [W]), wide("room%d_%d" % (h, j), [W]), wide("power%d_%d" % (h, j), [W]),
+                )
+                nc.vector.tensor_tensor(diff[:], table[:].indirect(listed[:, cols]), first[:], ALU.subtract)
+                nc.scalar.activation(out=room[:], in_=diff[:], func=ACT.Relu, scale=-1.0, bias=cap[:])
+                nc.scalar.activation(out=power[:], in_=room[:], func=ACT.Exp, scale=-1.0, bias=cap[:])
+                powers.append(power)
+            den = wide("den%d" % h, [W])
+            nc.vector.scalar_tensor_tensor(den[:], powers[0][:], 1.0, powers[1][:], ALU.add, ALU.add)
+            xs = wide("signed%d" % h, [2, 2, W // 4])
+            low = column("lowest%d" % h)
+            nc.vector.tensor_scalar(
+                xs[:].rearrange("p j m c -> p (j m c)"), den[:], lam_sign[:],
+                lowest[-1][:] if lowest else None, ALU.mult, ALU.min, accum_out=low[:],
+            )
+            signed.append(xs)
+            lowest.append(low)
+
+        inverse = []
+        for h in range(HALVES):
+            xs = signed[h]
+            pair = wide("pair%d" % h, [2, W // 4])
+            quad, quad_inv = wide("quad%d" % h, [W // 4]), wide("quad_inv%d" % h, [W // 4])
+            pair_inv = wide("pair_inv%d" % h, [2, W // 4])
+            inv = wide("inv%d" % h, [2, W // 2])
+            nc.vector.tensor_tensor(pair[:], xs[:, 0, :, :], xs[:, 1, :, :], ALU.mult)
+            nc.vector.tensor_tensor(quad[:], pair[:, 0, :], pair[:, 1, :], ALU.mult)
+            nc.vector.reciprocal(quad_inv[:], quad[:])
+            nc.vector.tensor_tensor(
+                pair_inv[:], pair[:, ::-1, :], quad_inv[:].unsqueeze(1).to_broadcast([P, 2, W // 4]), ALU.mult
+            )
+            nc.vector.tensor_tensor(
+                inv[:],
+                xs[:].rearrange("p j m c -> p j (m c)")[:, ::-1, :],
+                pair_inv[:].rearrange("p m c -> p (m c)").unsqueeze(1).to_broadcast([P, 2, W // 2]),
+                ALU.mult,
+            )
+            inverse.append(inv)
+
+        top, shift = column("top"), column("shift")
+        nc.vector.reciprocal(top[:], lowest[-1][:])
+        nc.vector.tensor_scalar(shift[:], top[:], lam_neg[:], None, ALU.mult)
+
+        shares, leans, sums, lean_sums = [], [], [], []
+        for h in range(HALVES):
+            inv = inverse[h][:].rearrange("p j c -> p (j c)")
+            p, t, tp = wide("p%d" % h, [W]), wide("t%d" % h, [W]), wide("tp%d" % h, [W])
+            z, l = column("z%d" % h), column("l%d" % h)
+            nc.scalar.activation(out=p[:], in_=inv, func=ACT.Exp, scale=lam_abs[:], bias=shift[:], accum_out=z[:])
+            nc.vector.tensor_scalar(t[:], inv, top[:], slope[:], ALU.subtract, ALU.mult)
+            nc.vector.scalar_tensor_tensor(tp[:], t[:], -1.0, p[:], ALU.add, ALU.mult, accum_out=l[:])
+            shares.append(p)
+            leans.append(t)
+            sums.append(z)
+            lean_sums.append(l)
+        total, total_inv, centre, gate = column("total"), column("total_inv"), column("centre"), column("gate")
+        nc.vector.tensor_tensor(total[:], sums[0][:], sums[1][:], ALU.add)
+        nc.vector.reciprocal(total_inv[:], total[:])
+        nc.vector.tensor_scalar(centre[:], lean_sums[0][:], lean_sums[1][:], total_inv[:], ALU.add, ALU.mult)
+        nc.gpsimd.tensor_tensor(gate[:], total_inv[:], gain128[:], ALU.mult)
+
+        for h in range(HALVES):
+            cols = slice(h * W, (h + 1) * W)
+            weight, gated, result = wide("weight%d" % h, [W]), wide("gated%d" % h, [W]), wide("result%d" % h, [W])
+            nc.vector.scalar_tensor_tensor(weight[:], leans[h][:], centre[:], shares[h][:], ALU.subtract, ALU.mult)
+            nc.scalar.activation(out=gated[:], in_=weight[:], func=ACT.Tanh, scale=gate[:])
+            nc.vector.tensor_tensor(result[:], gated[:], base_sb[:, cols], ALU.add)
+            nc.sync.dma_start(out=out[:, cols], in_=result[:])

@@ -22,7 +22,8 @@ W = I // HALVES
 LIST_COLS = W // 16
 A_PIECE = 256
 KEY_PIECE = 512
-CAP = 20.0
+CAP = 2.0**31
+OUT_PIECE = 128
 
 
 def tile_attend_quotaratio_leaning_gated_heads_kernel(
@@ -50,7 +51,7 @@ def tile_attend_quotaratio_leaning_gated_heads_kernel(
         words_hbm = keys_words[0].rearrange("p n t -> p (n t)")
         nc.sync.dma_start(out=raw[0][:], in_=query.rearrange("(p j) w -> p j w", j=PACK))
         for r in range(4):
-            nc.scalar.dma_start(
+            (nc.sync if r < 2 else nc.scalar).dma_start(
                 out=key_scales[r:P:32, :].bitcast(I32), in_=keys_scales[0][r:16:4, :].bitcast(I32)
             )
         for n in range(T // KEY_PIECE):
@@ -62,31 +63,22 @@ def tile_attend_quotaratio_leaning_gated_heads_kernel(
             tile = keep.tile([P, I // 16], U16, name=name)
             nc.sync.dma_start(tile[:], src)
             lists.append(tile)
+        nc.sync.dma_start(out=lam_sb[:], in_=lam)
+        nc.sync.dma_start(out=lean_sb[:], in_=lean)
+        nc.sync.dma_start(out=gain_sb[:], in_=gain2)
         base_sb = wide("base_sb", [I])
         nc.sync.dma_start(out=base_sb[:], in_=base)
-        nc.gpsimd.dma_start(out=lam_sb[:], in_=lam)
-        nc.gpsimd.dma_start(out=lean_sb[:], in_=lean)
-        nc.gpsimd.dma_start(out=gain_sb[:], in_=gain2)
-
-        cap = column("cap")
-        nc.gpsimd.memset(cap[:], CAP)
-        lam_abs, lam_neg, lam_ge, lam_sign = (
-            column("lam_abs"), column("lam_neg"), column("lam_ge"), column("lam_sign"),
-        )
-        slope, gain128 = column("slope"), column("gain128")
-        nc.scalar.activation(out=lam_abs[:], in_=lam_sb[:], func=ACT.Abs)
-        nc.gpsimd.tensor_scalar(lam_ge[:], lam_sb[:], 0.0, None, ALU.is_ge)
-        nc.gpsimd.tensor_scalar(lam_sign[:], lam_ge[:], 2.0, -1.0, ALU.mult, ALU.add)
-        nc.gpsimd.tensor_scalar(lam_neg[:], lam_abs[:], -1.0, 0.0, ALU.mult, ALU.add)
-        nc.gpsimd.tensor_tensor(slope[:], lam_abs[:], lean_sb[:], ALU.mult)
-        nc.gpsimd.tensor_scalar(gain128[:], gain_sb[:], 128.0, 0.0, ALU.mult, ALU.add)
 
         a_sb, b_sb = wide("a_sb", [T]), wide("b_sb", [T])
-        for n, (scores, piece) in enumerate(((a_sb, A_PIECE), (b_sb, KEY_PIECE))):
+        for n, (scores, piece) in enumerate(((a_sb, A_PIECE), (b_sb, A_PIECE))):
             grouped = keep.tile([P, Q, PACK], BF16, name="grouped%d" % n, align_bytes=64)
             codes = keep.tile([P, Q], U32, name="codes%d" % n, align_bytes=64)
             scales = keep.tile([P, Q], U8, name="scales%d" % n, align_bytes=64)
-            nc.vector.tensor_copy(out=grouped[:], in_=raw[n][:].rearrange("p j w -> p w j"))
+            interleaved = raw[n][:].rearrange("p j w -> p w j")
+            split = Q // 2 if n == 0 else 0
+            if split:
+                nc.vector.tensor_copy(out=grouped[:, :split, :], in_=interleaved[:, :split, :])
+            nc.scalar.copy(out=grouped[:, split:, :], in_=interleaved[:, split:, :])
             nc.vector.quantize_mx(
                 out=codes[:].bitcast(FP8X4), scales=scales[:], in_=grouped[:].rearrange("p w j -> p (w j)")
             )
@@ -103,84 +95,127 @@ def tile_attend_quotaratio_leaning_gated_heads_kernel(
                     start=True,
                     stop=True,
                 )
-                on_scalar = c % 2 == n
+                on_scalar = n == 1
                 if on_scalar:
                     nc.scalar.copy(out=scores[:, t0 : t0 + piece], in_=bank[:])
                 else:
                     nc.vector.tensor_copy(out=scores[:, t0 : t0 + piece], in_=bank[:])
 
-        signed, lowest = [], []
-        for h in range(HALVES):
-            cols = slice(h * LIST_COLS, (h + 1) * LIST_COLS)
-            first = wide("first%d" % h, [W])
-            nc.scalar.activation(out=first[:], in_=a_sb[:].indirect(lists[0][:, cols]), func=ACT.Copy)
-            powers = []
-            for j, (table, listed) in enumerate(((a_sb, lists[1]), (b_sb, lists[2]))):
-                diff, room, power = (
-                    wide("diff%d_%d" % (h, j), [W]), wide("room%d_%d" % (h, j), [W]), wide("power%d_%d" % (h, j), [W]),
+        firsts = [wide("first%d" % h, [W]) for h in range(HALVES)]
+        list_cols = [slice(h * LIST_COLS, (h + 1) * LIST_COLS) for h in range(HALVES)]
+        nc.vector.tensor_copy(firsts[0][:], a_sb[:].indirect(lists[0][:, list_cols[0]]))
+        nc.scalar.activation(out=firsts[1][:], in_=a_sb[:].indirect(lists[0][:, list_cols[1]]), func=ACT.Copy)
+        diffs = [[], []]
+        for j, (table, listed) in enumerate(((a_sb, lists[1]), (b_sb, lists[2]))):
+            for h in range(HALVES):
+                diff = wide("diff%d_%d" % (h, j), [W])
+                nc.vector.tensor_tensor(
+                    diff[:], table[:].indirect(listed[:, list_cols[h]]), firsts[h][:], ALU.subtract
                 )
-                nc.vector.tensor_tensor(diff[:], table[:].indirect(listed[:, cols]), first[:], ALU.subtract)
-                nc.scalar.activation(out=room[:], in_=diff[:], func=ACT.Relu, scale=-1.0, bias=cap[:])
-                nc.scalar.activation(out=power[:], in_=room[:], func=ACT.Exp, scale=-1.0, bias=cap[:])
-                powers.append(power)
-            den = wide("den%d" % h, [W])
-            nc.vector.scalar_tensor_tensor(den[:], powers[0][:], 1.0, powers[1][:], ALU.add, ALU.add)
-            xs = wide("signed%d" % h, [2, 2, W // 4])
-            low = column("lowest%d" % h)
-            nc.vector.tensor_scalar(
-                xs[:].rearrange("p j m c -> p (j m c)"), den[:], lam_sign[:],
-                lowest[-1][:] if lowest else None, ALU.mult, ALU.min, accum_out=low[:],
-            )
-            signed.append(xs)
-            lowest.append(low)
+                diffs[h].append(diff)
+        powers = [[], []]
+        for j in range(2):
+            for h in range(HALVES):
+                power = wide("power%d_%d" % (h, j), [W])
+                nc.scalar.activation(out=power[:], in_=diffs[h][j][:], func=ACT.Exp)
+                powers[h].append(power)
 
-        inverse = []
-        for h in range(HALVES):
-            xs = signed[h]
-            pair = wide("pair%d" % h, [2, W // 4])
-            quad, quad_inv = wide("quad%d" % h, [W // 4]), wide("quad_inv%d" % h, [W // 4])
-            pair_inv = wide("pair_inv%d" % h, [2, W // 4])
-            inv = wide("inv%d" % h, [2, W // 2])
-            nc.vector.tensor_tensor(pair[:], xs[:, 0, :, :], xs[:, 1, :, :], ALU.mult)
-            nc.vector.tensor_tensor(quad[:], pair[:, 0, :], pair[:, 1, :], ALU.mult)
-            nc.vector.reciprocal(quad_inv[:], quad[:])
-            nc.vector.tensor_tensor(
-                pair_inv[:], pair[:, ::-1, :], quad_inv[:].unsqueeze(1).to_broadcast([P, 2, W // 4]), ALU.mult
+        lam_sign, lam_neg, slope, gain128 = (
+            column("lam_sign"), column("lam_neg"), column("slope"), column("gain128"),
+        )
+        nc.vector.tensor_scalar(lam_sign[:], lam_sb[:], 0.0, -0.5, ALU.is_ge, ALU.add)
+        nc.vector.tensor_scalar(lam_neg[:], lam_sb[:], lam_sign[:], -1.0, ALU.mult, ALU.mult)
+        nc.scalar.activation(out=slope[:], in_=lean_sb[:], func=ACT.Identity, scale=lam_sb[:])
+        nc.scalar.activation(out=gain128[:], in_=gain_sb[:], func=ACT.Copy, scale=-128.0)
+
+        G = W // 4
+        raw_den = [wide("raw_den%d" % h, [W]) for h in range(HALVES)]
+        den = [wide("den%d" % h, [2, 2, G]) for h in range(HALVES)]
+        signed = [wide("signed%d" % h, [W]) for h in range(HALVES)]
+        lowest = [column("lowest%d" % h) for h in range(HALVES)]
+        pair = [wide("pair%d" % h, [2, G]) for h in range(HALVES)]
+        quad = [wide("quad%d" % h, [G]) for h in range(HALVES)]
+        quad_inv = [wide("quad_inv%d" % h, [G]) for h in range(HALVES)]
+        pair_inv = [wide("pair_inv%d" % h, [2, G]) for h in range(HALVES)]
+        inverse = [wide("inv%d" % h, [2, 2 * G]) for h in range(HALVES)]
+        top, shift = column("top"), column("shift")
+
+        def add_up(h):
+            nc.vector.scalar_tensor_tensor(raw_den[h][:], powers[h][0][:], 1.0, powers[h][1][:], ALU.add, ALU.add)
+
+        def limit(h):
+            nc.vector.tensor_scalar(den[h][:].rearrange("p j m c -> p (j m c)"), raw_den[h][:], CAP, None, ALU.min)
+
+        def sign_and_lowest(h):
+            nc.vector.tensor_scalar(
+                signed[h][:], raw_den[h][:], lam_sign[:],
+                lowest[h - 1][:] if h else None, ALU.mult, ALU.min, accum_out=lowest[h][:],
             )
+            if h == HALVES - 1:
+                nc.vector.reciprocal(top[:], lowest[h][:])
+                nc.scalar.activation(out=shift[:], in_=top[:], func=ACT.Identity, scale=lam_neg[:])
+
+        def pairs(h):
+            nc.vector.tensor_tensor(pair[h][:], den[h][:, 0, :, :], den[h][:, 1, :, :], ALU.mult)
+
+        def quads(h):
+            nc.vector.tensor_tensor(quad[h][:], pair[h][:, 0, :], pair[h][:, 1, :], ALU.mult)
+
+        def invert_quads(h):
+            nc.vector.reciprocal(quad_inv[h][:], quad[h][:])
+
+        def invert_pairs(h):
             nc.vector.tensor_tensor(
-                inv[:],
-                xs[:].rearrange("p j m c -> p j (m c)")[:, ::-1, :],
-                pair_inv[:].rearrange("p m c -> p (m c)").unsqueeze(1).to_broadcast([P, 2, W // 2]),
+                pair_inv[h][:], pair[h][:, ::-1, :], quad_inv[h][:].unsqueeze(1).to_broadcast([P, 2, G]), ALU.mult
+            )
+
+        def invert(h):
+            nc.vector.tensor_tensor(
+                inverse[h][:],
+                den[h][:].rearrange("p j m c -> p j (m c)")[:, ::-1, :],
+                pair_inv[h][:].rearrange("p m c -> p (m c)").unsqueeze(1).to_broadcast([P, 2, 2 * G]),
                 ALU.mult,
             )
-            inverse.append(inv)
 
-        top, shift = column("top"), column("shift")
-        nc.vector.reciprocal(top[:], lowest[-1][:])
-        nc.vector.tensor_scalar(shift[:], top[:], lam_neg[:], None, ALU.mult)
+        shares = [wide("p%d" % h, [W]) for h in range(HALVES)]
+        leaned = [wide("tp%d" % h, [W]) for h in range(HALVES)]
+        sums = [column("z%d" % h) for h in range(HALVES)]
+        lean_sums = [column("l%d" % h) for h in range(HALVES)]
 
-        shares, leans, sums, lean_sums = [], [], [], []
-        for h in range(HALVES):
-            inv = inverse[h][:].rearrange("p j c -> p (j c)")
-            p, t, tp = wide("p%d" % h, [W]), wide("t%d" % h, [W]), wide("tp%d" % h, [W])
-            z, l = column("z%d" % h), column("l%d" % h)
-            nc.scalar.activation(out=p[:], in_=inv, func=ACT.Exp, scale=lam_abs[:], bias=shift[:], accum_out=z[:])
-            nc.vector.tensor_scalar(t[:], inv, top[:], slope[:], ALU.subtract, ALU.mult)
-            nc.vector.scalar_tensor_tensor(tp[:], t[:], -1.0, p[:], ALU.add, ALU.mult, accum_out=l[:])
-            shares.append(p)
-            leans.append(t)
-            sums.append(z)
-            lean_sums.append(l)
+        def exponentiate(h):
+            nc.scalar.activation(
+                out=shares[h][:], in_=inverse[h][:].rearrange("p j c -> p (j c)"), func=ACT.Exp,
+                scale=lam_sb[:], bias=shift[:], accum_out=sums[h][:],
+            )
+
+        def lean_on(h):
+            nc.vector.scalar_tensor_tensor(
+                leaned[h][:], inverse[h][:].rearrange("p j c -> p (j c)"), slope[:], shares[h][:],
+                ALU.mult, ALU.mult, accum_out=lean_sums[h][:],
+            )
+
+        for step in (add_up, limit, pairs, quads, invert_quads, sign_and_lowest, invert_pairs, invert, exponentiate, lean_on):
+            for h in range(HALVES):
+                step(h)
+
         total, total_inv, centre, gate = column("total"), column("total_inv"), column("centre"), column("gate")
-        nc.vector.tensor_tensor(total[:], sums[0][:], sums[1][:], ALU.add)
+        rest = column("rest")
+        nc.scalar.activation(out=total[:], in_=sums[1][:], func=ACT.Identity, bias=sums[0][:])
+        nc.scalar.activation(out=rest[:], in_=lean_sums[0][:], func=ACT.Identity, scale=-1.0, bias=total[:])
         nc.vector.reciprocal(total_inv[:], total[:])
-        nc.vector.tensor_scalar(centre[:], lean_sums[0][:], lean_sums[1][:], total_inv[:], ALU.add, ALU.mult)
-        nc.gpsimd.tensor_tensor(gate[:], total_inv[:], gain128[:], ALU.mult)
+        nc.vector.tensor_scalar(centre[:], lean_sums[1][:], rest[:], total_inv[:], ALU.subtract, ALU.mult)
+        nc.scalar.activation(out=gate[:], in_=total_inv[:], func=ACT.Identity, scale=gain128[:])
 
-        for h in range(HALVES):
-            cols = slice(h * W, (h + 1) * W)
-            weight, gated, result = wide("weight%d" % h, [W]), wide("gated%d" % h, [W]), wide("result%d" % h, [W])
-            nc.vector.scalar_tensor_tensor(weight[:], leans[h][:], centre[:], shares[h][:], ALU.subtract, ALU.mult)
+        for c in range(I // OUT_PIECE):
+            cols = slice(c * OUT_PIECE, (c + 1) * OUT_PIECE)
+            h, start = divmod(c * OUT_PIECE, W)
+            within = slice(start, start + OUT_PIECE)
+            weight, gated, result = (
+                wide("weight%d" % c, [OUT_PIECE]), wide("gated%d" % c, [OUT_PIECE]), wide("result%d" % c, [OUT_PIECE]),
+            )
+            nc.vector.scalar_tensor_tensor(
+                weight[:], shares[h][:, within], centre[:], leaned[h][:, within], ALU.mult, ALU.subtract
+            )
             nc.scalar.activation(out=gated[:], in_=weight[:], func=ACT.Tanh, scale=gate[:])
             nc.vector.tensor_tensor(result[:], gated[:], base_sb[:, cols], ALU.add)
             nc.sync.dma_start(out=out[:, cols], in_=result[:])

@@ -34,11 +34,11 @@ def tile_attend_quotaratio_leaning_gated_heads_kernel(
         keep = ctx.enter_context(tc.tile_pool(name="keep", bufs=1))
         psum = ctx.enter_context(tc.psum_pool(name="psum", bufs=1))
 
-        def column(name):
-            return keep.tile([P, 1], F32, name=name)
+        def column(name, tag=None):
+            return keep.tile([P, 1], F32, name=name, tag=tag or name)
 
         def wide(name, shape):
-            return keep.tile([P] + shape, F32, name=name)
+            return keep.tile([P] + shape, F32, name=name, tag=name)
 
         lam_sb, lean_sb, gain_sb = column("lam_sb"), column("lean_sb"), column("gain_sb")
         key_scales = keep.tile([P, T], U8, name="key_scales", align_bytes=64)
@@ -95,7 +95,7 @@ def tile_attend_quotaratio_leaning_gated_heads_kernel(
                     start=True,
                     stop=True,
                 )
-                on_scalar = n == 1
+                on_scalar = n == 1 or c == 0
                 if on_scalar:
                     nc.scalar.copy(out=scores[:, t0 : t0 + piece], in_=bank[:])
                 else:
@@ -120,11 +120,11 @@ def tile_attend_quotaratio_leaning_gated_heads_kernel(
                 nc.scalar.activation(out=power[:], in_=diffs[h][j][:], func=ACT.Exp)
                 powers[h].append(power)
 
-        lam_sign, lam_neg, slope, gain128 = (
-            column("lam_sign"), column("lam_neg"), column("slope"), column("gain128"),
-        )
-        nc.vector.tensor_scalar(lam_sign[:], lam_sb[:], 0.0, -0.5, ALU.is_ge, ALU.add)
-        nc.vector.tensor_scalar(lam_neg[:], lam_sb[:], lam_sign[:], -1.0, ALU.mult, ALU.mult)
+        lam_sign, flip = column("lam_sign", "diff1_0"), column("flip")
+        lam_abs, slope, gain128 = column("lam_abs", "diff0_0"), column("slope", "diff0_1"), column("gain128", "diff1_1")
+        nc.scalar.activation(out=lam_sign[:], in_=lam_sb[:], func=ACT.Sign)
+        nc.scalar.activation(out=flip[:], in_=lam_sign[:], func=ACT.Sign, scale=-1.0, bias=-0.5)
+        nc.scalar.activation(out=lam_abs[:], in_=lam_sb[:], func=ACT.Abs)
         nc.scalar.activation(out=slope[:], in_=lean_sb[:], func=ACT.Identity, scale=lam_sb[:])
         nc.scalar.activation(out=gain128[:], in_=gain_sb[:], func=ACT.Copy, scale=-128.0)
 
@@ -148,12 +148,12 @@ def tile_attend_quotaratio_leaning_gated_heads_kernel(
 
         def sign_and_lowest(h):
             nc.vector.tensor_scalar(
-                signed[h][:], raw_den[h][:], lam_sign[:],
-                lowest[h - 1][:] if h else None, ALU.mult, ALU.min, accum_out=lowest[h][:],
+                signed[h][:], raw_den[h][:], flip[:],
+                lowest[h - 1][:] if h else None, ALU.mult, ALU.max, accum_out=lowest[h][:],
             )
             if h == HALVES - 1:
                 nc.vector.reciprocal(top[:], lowest[h][:])
-                nc.scalar.activation(out=shift[:], in_=top[:], func=ACT.Identity, scale=lam_neg[:])
+                nc.scalar.activation(out=shift[:], in_=top[:], func=ACT.Identity, scale=lam_abs[:])
 
         def pairs(h):
             nc.vector.tensor_tensor(pair[h][:], den[h][:, 0, :, :], den[h][:, 1, :, :], ALU.mult)

@@ -17,13 +17,17 @@ ACT = mybir.ActivationFunctionType
 
 P = 128
 PACK = 4
+LIST_ROWS = 16
+SCALE_ROWS = 4
 HALVES = 2
 W = I // HALVES
-LIST_COLS = W // 16
-A_PIECE = 256
+QUADS = W // 4
 KEY_PIECE = 512
-CAP = 2.0**31
+A_PIECES = (256, 256, 256, 128, 128)
+B_PIECES = (512, 256, 256)
+A_ON_VECTOR = (0, 3)
 OUT_PIECE = 128
+DEN_LIMIT = 2.0**31
 
 
 def tile_attend_quotaratio_leaning_gated_heads_kernel(
@@ -40,29 +44,31 @@ def tile_attend_quotaratio_leaning_gated_heads_kernel(
         def wide(name, shape):
             return keep.tile([P] + shape, F32, name=name, tag=name)
 
+        def by_half(name, shape):
+            return [wide("%s%d" % (name, h), shape) for h in range(HALVES)]
+
         lam_sb, lean_sb, gain_sb = column("lam_sb"), column("lean_sb"), column("gain_sb")
         key_scales = keep.tile([P, T], U8, name="key_scales", align_bytes=64)
-
-        raw = [wide("raw_q%d" % n, [PACK, Q]) for n in range(2)]
+        raw_queries = [wide("raw_query%d" % n, [PACK, Q]) for n in range(2)]
         key_words = [
-            keep.tile([P, KEY_PIECE], U32, name="key_words%d" % n, align_bytes=64)
-            for n in range(T // KEY_PIECE)
+            keep.tile([P, KEY_PIECE], U32, name="key_words%d" % n, align_bytes=64) for n in range(T // KEY_PIECE)
         ]
         words_hbm = keys_words[0].rearrange("p n t -> p (n t)")
-        nc.sync.dma_start(out=raw[0][:], in_=query.rearrange("(p j) w -> p j w", j=PACK))
-        for r in range(4):
-            (nc.sync if r < 2 else nc.scalar).dma_start(
-                out=key_scales[r:P:32, :].bitcast(I32), in_=keys_scales[0][r:16:4, :].bitcast(I32)
+        nc.sync.dma_start(out=raw_queries[0][:], in_=query.rearrange("(p j) w -> p j w", j=PACK))
+        for r in range(SCALE_ROWS):
+            (nc.sync if r < SCALE_ROWS // 2 else nc.scalar).dma_start(
+                out=key_scales[r:P:32, :].bitcast(I32),
+                in_=keys_scales[0][r : D // 32 : SCALE_ROWS, :].bitcast(I32),
             )
         for n in range(T // KEY_PIECE):
-            piece = slice(n * KEY_PIECE * PACK, (n + 1) * KEY_PIECE * PACK)
-            nc.sync.dma_start(out=key_words[n][:].bitcast(I32), in_=words_hbm[:, piece].bitcast(I32))
-        nc.sync.dma_start(out=raw[1][:], in_=query2.rearrange("(p j) w -> p j w", j=PACK))
+            word_bytes = slice(n * KEY_PIECE * PACK, (n + 1) * KEY_PIECE * PACK)
+            nc.sync.dma_start(out=key_words[n][:].bitcast(I32), in_=words_hbm[:, word_bytes].bitcast(I32))
+        nc.sync.dma_start(out=raw_queries[1][:], in_=query2.rearrange("(p j) w -> p j w", j=PACK))
         lists = []
-        for name, src in (("offs_sb", offs), ("offs2_sb", offs2), ("offs3_sb", offs3)):
-            tile = keep.tile([P, I // 16], U16, name=name)
-            nc.sync.dma_start(tile[:], src)
-            lists.append(tile)
+        for name, listed_hbm in (("offs_sb", offs), ("offs2_sb", offs2), ("offs3_sb", offs3)):
+            listed = keep.tile([P, I // LIST_ROWS], U16, name=name)
+            nc.sync.dma_start(listed[:], listed_hbm)
+            lists.append(listed)
         nc.sync.dma_start(out=lam_sb[:], in_=lam)
         nc.sync.dma_start(out=lean_sb[:], in_=lean)
         nc.sync.dma_start(out=gain_sb[:], in_=gain2)
@@ -70,48 +76,45 @@ def tile_attend_quotaratio_leaning_gated_heads_kernel(
         nc.sync.dma_start(out=base_sb[:], in_=base)
 
         a_sb, b_sb = wide("a_sb", [T]), wide("b_sb", [T])
-        for n, (scores, piece) in enumerate(((a_sb, A_PIECE), (b_sb, A_PIECE))):
+        for n, (scores, pieces) in enumerate(((a_sb, A_PIECES), (b_sb, B_PIECES))):
             grouped = keep.tile([P, Q, PACK], BF16, name="grouped%d" % n, align_bytes=64)
             codes = keep.tile([P, Q], U32, name="codes%d" % n, align_bytes=64)
             scales = keep.tile([P, Q], U8, name="scales%d" % n, align_bytes=64)
-            interleaved = raw[n][:].rearrange("p j w -> p w j")
-            split = Q // 2 if n == 0 else 0
-            if split:
-                nc.vector.tensor_copy(out=grouped[:, :split, :], in_=interleaved[:, :split, :])
-            nc.scalar.copy(out=grouped[:, split:, :], in_=interleaved[:, split:, :])
+            interleaved = raw_queries[n][:].rearrange("p j w -> p w j")
+            split = Q // 2 if n == 0 else Q
+            nc.vector.tensor_copy(out=grouped[:, :split, :], in_=interleaved[:, :split, :])
+            if split < Q:
+                nc.scalar.copy(out=grouped[:, split:, :], in_=interleaved[:, split:, :])
             nc.vector.quantize_mx(
                 out=codes[:].bitcast(FP8X4), scales=scales[:], in_=grouped[:].rearrange("p w j -> p (w j)")
             )
-            for c in range(T // piece):
-                t0 = c * piece
+            for c, piece in enumerate(pieces):
+                t0 = sum(pieces[:c])
                 bank = psum.tile([P, piece], F32, name="bank%d_%d" % (n, c))
-                within = slice(t0 % KEY_PIECE, t0 % KEY_PIECE + piece)
+                within_load = slice(t0 % KEY_PIECE, t0 % KEY_PIECE + piece)
                 nc.tensor.matmul_mx(
                     out=bank[:],
                     lhsT=codes[:].bitcast(FP8X4),
                     lhsT_scale=scales[:],
-                    rhs=key_words[t0 // KEY_PIECE][:, within].bitcast(FP8X4),
+                    rhs=key_words[t0 // KEY_PIECE][:, within_load].bitcast(FP8X4),
                     rhs_scale=key_scales[:, t0 : t0 + piece],
                     start=True,
                     stop=True,
                 )
-                on_scalar = n == 1 or c == 0
-                if on_scalar:
-                    nc.scalar.copy(out=scores[:, t0 : t0 + piece], in_=bank[:])
-                else:
+                if n == 0 and c in A_ON_VECTOR:
                     nc.vector.tensor_copy(out=scores[:, t0 : t0 + piece], in_=bank[:])
+                else:
+                    nc.scalar.copy(out=scores[:, t0 : t0 + piece], in_=bank[:])
 
-        firsts = [wide("first%d" % h, [W]) for h in range(HALVES)]
-        list_cols = [slice(h * LIST_COLS, (h + 1) * LIST_COLS) for h in range(HALVES)]
-        nc.vector.tensor_copy(firsts[0][:], a_sb[:].indirect(lists[0][:, list_cols[0]]))
-        nc.scalar.activation(out=firsts[1][:], in_=a_sb[:].indirect(lists[0][:, list_cols[1]]), func=ACT.Copy)
+        a1 = by_half("a1_", [W])
+        list_cols = [slice(h * W // LIST_ROWS, (h + 1) * W // LIST_ROWS) for h in range(HALVES)]
+        nc.vector.tensor_copy(a1[0][:], a_sb[:].indirect(lists[0][:, list_cols[0]]))
+        nc.scalar.activation(out=a1[1][:], in_=a_sb[:].indirect(lists[0][:, list_cols[1]]), func=ACT.Copy)
         diffs = [[], []]
         for j, (table, listed) in enumerate(((a_sb, lists[1]), (b_sb, lists[2]))):
             for h in range(HALVES):
                 diff = wide("diff%d_%d" % (h, j), [W])
-                nc.vector.tensor_tensor(
-                    diff[:], table[:].indirect(listed[:, list_cols[h]]), firsts[h][:], ALU.subtract
-                )
+                nc.vector.tensor_tensor(diff[:], table[:].indirect(listed[:, list_cols[h]]), a1[h][:], ALU.subtract)
                 diffs[h].append(diff)
         powers = [[], []]
         for j in range(2):
@@ -128,93 +131,98 @@ def tile_attend_quotaratio_leaning_gated_heads_kernel(
         nc.scalar.activation(out=slope[:], in_=lean_sb[:], func=ACT.Identity, scale=lam_sb[:])
         nc.scalar.activation(out=gain128[:], in_=gain_sb[:], func=ACT.Copy, scale=-128.0)
 
-        G = W // 4
-        raw_den = [wide("raw_den%d" % h, [W]) for h in range(HALVES)]
-        den = [wide("den%d" % h, [2, 2, G]) for h in range(HALVES)]
-        signed = [wide("signed%d" % h, [W]) for h in range(HALVES)]
-        lowest = [column("lowest%d" % h) for h in range(HALVES)]
-        pair = [wide("pair%d" % h, [2, G]) for h in range(HALVES)]
-        quad = [wide("quad%d" % h, [G]) for h in range(HALVES)]
-        quad_inv = [wide("quad_inv%d" % h, [G]) for h in range(HALVES)]
-        pair_inv = [wide("pair_inv%d" % h, [2, G]) for h in range(HALVES)]
-        inverse = [wide("inv%d" % h, [2, 2 * G]) for h in range(HALVES)]
-        top, shift = column("top"), column("shift")
+        den = by_half("den", [3, 2 * QUADS])
+        den_slots = [den[h][:, 1:3, :].rearrange("p j c -> p (j c)") for h in range(HALVES)]
+        flipped = by_half("flipped", [W])
+        extreme = [column("extreme%d" % h) for h in range(HALVES)]
+        pair = by_half("pair", [2, QUADS])
+        quad = by_half("quad", [QUADS])
+        quad_inv = by_half("quad_inv", [QUADS])
+        pair_inv = by_half("pair_inv", [2, QUADS])
+        den_inv = by_half("den_inv", [2, 2 * QUADS])
+        extreme_inv, shift = column("extreme_inv"), column("shift")
+        shares = by_half("shares", [W])
+        leaned = by_half("leaned", [W])
+        share_sums = [column("share_sum%d" % h) for h in range(HALVES)]
+        leaned_sums = [column("leaned_sum%d" % h) for h in range(HALVES)]
 
         def add_up(h):
-            nc.vector.scalar_tensor_tensor(raw_den[h][:], powers[h][0][:], 1.0, powers[h][1][:], ALU.add, ALU.add)
+            nc.vector.scalar_tensor_tensor(den_slots[h], powers[h][0][:], 1.0, powers[h][1][:], ALU.add, ALU.add)
 
         def limit(h):
-            nc.vector.tensor_scalar(den[h][:].rearrange("p j m c -> p (j m c)"), raw_den[h][:], CAP, None, ALU.min)
+            nc.vector.tensor_scalar(den[h][:, 0, :], den[h][:, 2, :], DEN_LIMIT, None, ALU.min)
 
-        def sign_and_lowest(h):
-            nc.vector.tensor_scalar(
-                signed[h][:], raw_den[h][:], flip[:],
-                lowest[h - 1][:] if h else None, ALU.mult, ALU.max, accum_out=lowest[h][:],
+        def multiply_pairs(h):
+            nc.vector.scalar_tensor_tensor(
+                pair[h][:].rearrange("p m c -> p (m c)"), den[h][:, 1, :], DEN_LIMIT, den[h][:, 0, :], ALU.min, ALU.mult
             )
-            if h == HALVES - 1:
-                nc.vector.reciprocal(top[:], lowest[h][:])
-                nc.scalar.activation(out=shift[:], in_=top[:], func=ACT.Identity, scale=lam_abs[:])
 
-        def pairs(h):
-            nc.vector.tensor_tensor(pair[h][:], den[h][:, 0, :, :], den[h][:, 1, :, :], ALU.mult)
-
-        def quads(h):
+        def multiply_quads(h):
             nc.vector.tensor_tensor(quad[h][:], pair[h][:, 0, :], pair[h][:, 1, :], ALU.mult)
 
         def invert_quads(h):
             nc.vector.reciprocal(quad_inv[h][:], quad[h][:])
 
+        def find_largest_score(h):
+            nc.vector.tensor_scalar(
+                flipped[h][:], den_slots[h], flip[:], extreme[h - 1][:] if h else None,
+                ALU.mult, ALU.max, accum_out=extreme[h][:],
+            )
+            if h == HALVES - 1:
+                nc.vector.reciprocal(extreme_inv[:], extreme[h][:])
+                nc.scalar.activation(out=shift[:], in_=extreme_inv[:], func=ACT.Identity, scale=lam_abs[:])
+
         def invert_pairs(h):
             nc.vector.tensor_tensor(
-                pair_inv[h][:], pair[h][:, ::-1, :], quad_inv[h][:].unsqueeze(1).to_broadcast([P, 2, G]), ALU.mult
+                pair_inv[h][:], pair[h][:, ::-1, :], quad_inv[h][:].unsqueeze(1).to_broadcast([P, 2, QUADS]), ALU.mult
             )
 
-        def invert(h):
-            nc.vector.tensor_tensor(
-                inverse[h][:],
-                den[h][:].rearrange("p j m c -> p j (m c)")[:, ::-1, :],
-                pair_inv[h][:].rearrange("p m c -> p (m c)").unsqueeze(1).to_broadcast([P, 2, 2 * G]),
+        def invert_slots(h):
+            nc.vector.scalar_tensor_tensor(
+                den_inv[h][:],
+                den[h][:, 0:2, :],
+                DEN_LIMIT,
+                pair_inv[h][:].rearrange("p m c -> p (m c)").unsqueeze(1).to_broadcast([P, 2, 2 * QUADS]),
+                ALU.min,
                 ALU.mult,
             )
 
-        shares = [wide("p%d" % h, [W]) for h in range(HALVES)]
-        leaned = [wide("tp%d" % h, [W]) for h in range(HALVES)]
-        sums = [column("z%d" % h) for h in range(HALVES)]
-        lean_sums = [column("l%d" % h) for h in range(HALVES)]
-
         def exponentiate(h):
             nc.scalar.activation(
-                out=shares[h][:], in_=inverse[h][:].rearrange("p j c -> p (j c)"), func=ACT.Exp,
-                scale=lam_sb[:], bias=shift[:], accum_out=sums[h][:],
+                out=shares[h][:], in_=den_inv[h][:].rearrange("p j c -> p (j c)"), func=ACT.Exp,
+                scale=lam_sb[:], bias=shift[:], accum_out=share_sums[h][:],
             )
 
         def lean_on(h):
             nc.vector.scalar_tensor_tensor(
-                leaned[h][:], inverse[h][:].rearrange("p j c -> p (j c)"), slope[:], shares[h][:],
-                ALU.mult, ALU.mult, accum_out=lean_sums[h][:],
+                leaned[h][:], den_inv[h][:].rearrange("p j c -> p (j c)"), slope[:], shares[h][:],
+                ALU.mult, ALU.mult, accum_out=leaned_sums[h][:],
             )
 
-        for step in (add_up, limit, pairs, quads, invert_quads, sign_and_lowest, invert_pairs, invert, exponentiate, lean_on):
+        for step in (
+            add_up, limit, multiply_pairs, multiply_quads, invert_quads, find_largest_score,
+            invert_pairs, invert_slots, exponentiate, lean_on,
+        ):
             for h in range(HALVES):
                 step(h)
 
         total, total_inv, centre, gate = column("total"), column("total_inv"), column("centre"), column("gate")
         rest = column("rest")
-        nc.scalar.activation(out=total[:], in_=sums[1][:], func=ACT.Identity, bias=sums[0][:])
-        nc.scalar.activation(out=rest[:], in_=lean_sums[0][:], func=ACT.Identity, scale=-1.0, bias=total[:])
+        nc.scalar.activation(out=total[:], in_=share_sums[1][:], func=ACT.Identity, bias=share_sums[0][:])
+        nc.scalar.activation(out=rest[:], in_=leaned_sums[0][:], func=ACT.Identity, scale=-1.0, bias=total[:])
         nc.vector.reciprocal(total_inv[:], total[:])
-        nc.vector.tensor_scalar(centre[:], lean_sums[1][:], rest[:], total_inv[:], ALU.subtract, ALU.mult)
+        nc.vector.tensor_scalar(centre[:], leaned_sums[1][:], rest[:], total_inv[:], ALU.subtract, ALU.mult)
         nc.scalar.activation(out=gate[:], in_=total_inv[:], func=ACT.Identity, scale=gain128[:])
 
         for c in range(I // OUT_PIECE):
             cols = slice(c * OUT_PIECE, (c + 1) * OUT_PIECE)
             h, start = divmod(c * OUT_PIECE, W)
-            within = slice(start, start + OUT_PIECE)
+            within_half = slice(start, start + OUT_PIECE)
             weight, gated, result = (
                 wide("weight%d" % c, [OUT_PIECE]), wide("gated%d" % c, [OUT_PIECE]), wide("result%d" % c, [OUT_PIECE]),
             )
             nc.vector.scalar_tensor_tensor(
-                weight[:], shares[h][:, within], centre[:], leaned[h][:, within], ALU.mult, ALU.subtract
+                weight[:], shares[h][:, within_half], centre[:], leaned[h][:, within_half], ALU.mult, ALU.subtract
             )
             nc.scalar.activation(out=gated[:], in_=weight[:], func=ACT.Tanh, scale=gate[:])
             nc.vector.tensor_tensor(result[:], gated[:], base_sb[:, cols], ALU.add)

from contextlib import ExitStack

import concourse.mybir as mybir

D, T, I, Q = 512, 1024, 512, 128
FLOPS = 2 * 2 * D * T * Q

F32 = mybir.dt.float32
BF16 = mybir.dt.bfloat16
I32 = mybir.dt.int32
U32 = mybir.dt.uint32
U16 = mybir.dt.uint16
U8 = mybir.dt.uint8
FP8X4 = mybir.dt.float8_e4m3fn_x4
ALU = mybir.AluOpType
ACT = mybir.ActivationFunctionType

P = 128
PACK = 4
LIST_ROWS = 16
SCALE_ROWS = 4
HALVES = 2
W = I // HALVES
QUADS = W // 4
KEY_PIECE = 512
A_PIECES = (256, 256, 256, 128, 128)
B_PIECES = (512, 256, 256)
A_ON_VECTOR = (0, 3)
OUT_PIECE = 128
DEN_LIMIT = 2.0**31


def tile_attend_quotaratio_leaning_gated_heads_kernel(
    tc, query, query2, keys_words, keys_scales, lam, lean, base, gain2, offs, offs2, offs3, out
):
    nc = tc.nc
    with ExitStack() as ctx:
        keep = ctx.enter_context(tc.tile_pool(name="keep", bufs=1))
        psum = ctx.enter_context(tc.psum_pool(name="psum", bufs=1))

        def column(name, tag=None):
            return keep.tile([P, 1], F32, name=name, tag=tag or name)

        def wide(name, shape):
            return keep.tile([P] + shape, F32, name=name, tag=name)

        def by_half(name, shape):
            return [wide("%s%d" % (name, h), shape) for h in range(HALVES)]

        lam_sb, lean_sb, gain_sb = column("lam_sb"), column("lean_sb"), column("gain_sb")
        key_scales = keep.tile([P, T], U8, name="key_scales", align_bytes=64)
        raw_queries = [wide("raw_query%d" % n, [PACK, Q]) for n in range(2)]
        key_words = [
            keep.tile([P, KEY_PIECE], U32, name="key_words%d" % n, align_bytes=64) for n in range(T // KEY_PIECE)
        ]
        words_hbm = keys_words[0].rearrange("p n t -> p (n t)")
        nc.sync.dma_start(out=raw_queries[0][:], in_=query.rearrange("(p j) w -> p j w", j=PACK))
        for r in range(SCALE_ROWS):
            (nc.sync if r < SCALE_ROWS // 2 else nc.scalar).dma_start(
                out=key_scales[r:P:32, :].bitcast(I32),
                in_=keys_scales[0][r : D // 32 : SCALE_ROWS, :].bitcast(I32),
            )
        for n in range(T // KEY_PIECE):
            word_bytes = slice(n * KEY_PIECE * PACK, (n + 1) * KEY_PIECE * PACK)
            nc.sync.dma_start(out=key_words[n][:].bitcast(I32), in_=words_hbm[:, word_bytes].bitcast(I32))
        nc.sync.dma_start(out=raw_queries[1][:], in_=query2.rearrange("(p j) w -> p j w", j=PACK))
        lists = []
        for name, listed_hbm in (("offs_sb", offs), ("offs2_sb", offs2), ("offs3_sb", offs3)):
            listed = keep.tile([P, I // LIST_ROWS], U16, name=name)
            nc.sync.dma_start(listed[:], listed_hbm)
            lists.append(listed)
        nc.sync.dma_start(out=lam_sb[:], in_=lam)
        nc.sync.dma_start(out=lean_sb[:], in_=lean)
        nc.sync.dma_start(out=gain_sb[:], in_=gain2)
        base_sb = wide("base_sb", [I])
        nc.sync.dma_start(out=base_sb[:], in_=base)

        a_sb, b_sb = wide("a_sb", [T]), wide("b_sb", [T])
        for n, (scores, pieces) in enumerate(((a_sb, A_PIECES), (b_sb, B_PIECES))):
            grouped = keep.tile([P, Q, PACK], BF16, name="grouped%d" % n, align_bytes=64)
            codes = keep.tile([P, Q], U32, name="codes%d" % n, align_bytes=64)
            scales = keep.tile([P, Q], U8, name="scales%d" % n, align_bytes=64)
            interleaved = raw_queries[n][:].rearrange("p j w -> p w j")
            split = Q // 2 if n == 0 else Q
            nc.vector.tensor_copy(out=grouped[:, :split, :], in_=interleaved[:, :split, :])
            if split < Q:
                nc.scalar.copy(out=grouped[:, split:, :], in_=interleaved[:, split:, :])
            nc.vector.quantize_mx(
                out=codes[:].bitcast(FP8X4), scales=scales[:], in_=grouped[:].rearrange("p w j -> p (w j)")
            )
            for c, piece in enumerate(pieces):
                t0 = sum(pieces[:c])
                bank = psum.tile([P, piece], F32, name="bank%d_%d" % (n, c))
                within_load = slice(t0 % KEY_PIECE, t0 % KEY_PIECE + piece)
                nc.tensor.matmul_mx(
                    out=bank[:],
                    lhsT=codes[:].bitcast(FP8X4),
                    lhsT_scale=scales[:],
                    rhs=key_words[t0 // KEY_PIECE][:, within_load].bitcast(FP8X4),
                    rhs_scale=key_scales[:, t0 : t0 + piece],
                    start=True,
                    stop=True,
                )
                if n == 0 and c in A_ON_VECTOR:
                    nc.vector.tensor_copy(out=scores[:, t0 : t0 + piece], in_=bank[:])
                else:
                    nc.scalar.copy(out=scores[:, t0 : t0 + piece], in_=bank[:])

        a1 = by_half("a1_", [W])
        list_cols = [slice(h * W // LIST_ROWS, (h + 1) * W // LIST_ROWS) for h in range(HALVES)]
        nc.vector.tensor_copy(a1[0][:], a_sb[:].indirect(lists[0][:, list_cols[0]]))
        nc.scalar.activation(out=a1[1][:], in_=a_sb[:].indirect(lists[0][:, list_cols[1]]), func=ACT.Copy)
        diffs = [[], []]
        for j, (table, listed) in enumerate(((a_sb, lists[1]), (b_sb, lists[2]))):
            for h in range(HALVES):
                diff = wide("diff%d_%d" % (h, j), [W])
                nc.vector.tensor_tensor(diff[:], table[:].indirect(listed[:, list_cols[h]]), a1[h][:], ALU.subtract)
                diffs[h].append(diff)
        powers = [[], []]
        for j in range(2):
            for h in range(HALVES):
                power = wide("power%d_%d" % (h, j), [W])
                nc.scalar.activation(out=power[:], in_=diffs[h][j][:], func=ACT.Exp)
                powers[h].append(power)

        lam_sign, flip = column("lam_sign", "diff1_0"), column("flip")
        lam_abs, slope, gain128 = column("lam_abs", "diff0_0"), column("slope", "diff0_1"), column("gain128", "diff1_1")
        nc.scalar.activation(out=lam_sign[:], in_=lam_sb[:], func=ACT.Sign)
        nc.scalar.activation(out=flip[:], in_=lam_sign[:], func=ACT.Sign, scale=-1.0, bias=-0.5)
        nc.scalar.activation(out=lam_abs[:], in_=lam_sb[:], func=ACT.Abs)
        nc.scalar.activation(out=slope[:], in_=lean_sb[:], func=ACT.Identity, scale=lam_sb[:])
        nc.scalar.activation(out=gain128[:], in_=gain_sb[:], func=ACT.Copy, scale=-128.0)

        den = by_half("den", [3, 2 * QUADS])
        den_slots = [den[h][:, 1:3, :].rearrange("p j c -> p (j c)") for h in range(HALVES)]
        flipped = by_half("flipped", [W])
        extreme = [column("extreme%d" % h) for h in range(HALVES)]
        pair = by_half("pair", [2, QUADS])
        quad = by_half("quad", [QUADS])
        quad_inv = by_half("quad_inv", [QUADS])
        pair_inv = by_half("pair_inv", [2, QUADS])
        den_inv = by_half("den_inv", [2, 2 * QUADS])
        extreme_inv, shift = column("extreme_inv"), column("shift")
        shares = by_half("shares", [W])
        leaned = by_half("leaned", [W])
        share_sums = [column("share_sum%d" % h) for h in range(HALVES)]
        leaned_sums = [column("leaned_sum%d" % h) for h in range(HALVES)]

        def add_up(h):
            nc.vector.scalar_tensor_tensor(den_slots[h], powers[h][0][:], 1.0, powers[h][1][:], ALU.add, ALU.add)

        def limit(h):
            nc.vector.tensor_scalar(den[h][:, 0, :], den[h][:, 2, :], DEN_LIMIT, None, ALU.min)

        def multiply_pairs(h):
            nc.vector.scalar_tensor_tensor(
                pair[h][:].rearrange("p m c -> p (m c)"), den[h][:, 1, :], DEN_LIMIT, den[h][:, 0, :], ALU.min, ALU.mult
            )

        def multiply_quads(h):
            nc.vector.tensor_tensor(quad[h][:], pair[h][:, 0, :], pair[h][:, 1, :], ALU.mult)

        def invert_quads(h):
            nc.vector.reciprocal(quad_inv[h][:], quad[h][:])

        def find_largest_score(h):
            nc.vector.tensor_scalar(
                flipped[h][:], den_slots[h], flip[:], extreme[h - 1][:] if h else None,
                ALU.mult, ALU.max, accum_out=extreme[h][:],
            )
            if h == HALVES - 1:
                nc.vector.reciprocal(extreme_inv[:], extreme[h][:])
                nc.scalar.activation(out=shift[:], in_=extreme_inv[:], func=ACT.Identity, scale=lam_abs[:])

        def invert_pairs(h):
            nc.vector.tensor_tensor(
                pair_inv[h][:], pair[h][:, ::-1, :], quad_inv[h][:].unsqueeze(1).to_broadcast([P, 2, QUADS]), ALU.mult
            )

        def invert_slots(h):
            nc.vector.scalar_tensor_tensor(
                den_inv[h][:],
                den[h][:, 0:2, :],
                DEN_LIMIT,
                pair_inv[h][:].rearrange("p m c -> p (m c)").unsqueeze(1).to_broadcast([P, 2, 2 * QUADS]),
                ALU.min,
                ALU.mult,
            )

        def exponentiate(h):
            nc.scalar.activation(
                out=shares[h][:], in_=den_inv[h][:].rearrange("p j c -> p (j c)"), func=ACT.Exp,
                scale=lam_sb[:], bias=shift[:], accum_out=share_sums[h][:],
            )

        def lean_on(h):
            nc.vector.scalar_tensor_tensor(
                leaned[h][:], den_inv[h][:].rearrange("p j c -> p (j c)"), slope[:], shares[h][:],
                ALU.mult, ALU.mult, accum_out=leaned_sums[h][:],
            )

        for step in (
            add_up, limit, multiply_pairs, multiply_quads, invert_quads, find_largest_score,
            invert_pairs, invert_slots, exponentiate, lean_on,
        ):
            for h in range(HALVES):
                step(h)

        total, total_inv, centre, gate = column("total"), column("total_inv"), column("centre"), column("gate")
        rest = column("rest")
        nc.scalar.activation(out=total[:], in_=share_sums[1][:], func=ACT.Identity, bias=share_sums[0][:])
        nc.scalar.activation(out=rest[:], in_=leaned_sums[0][:], func=ACT.Identity, scale=-1.0, bias=total[:])
        nc.vector.reciprocal(total_inv[:], total[:])
        nc.vector.tensor_scalar(centre[:], leaned_sums[1][:], rest[:], total_inv[:], ALU.subtract, ALU.mult)
        nc.scalar.activation(out=gate[:], in_=total_inv[:], func=ACT.Identity, scale=gain128[:])

        for c in range(I // OUT_PIECE):
            cols = slice(c * OUT_PIECE, (c + 1) * OUT_PIECE)
            h, start = divmod(c * OUT_PIECE, W)
            within_half = slice(start, start + OUT_PIECE)
            weight, gated, result = (
                wide("weight%d" % c, [OUT_PIECE]), wide("gated%d" % c, [OUT_PIECE]), wide("result%d" % c, [OUT_PIECE]),
            )
            nc.vector.scalar_tensor_tensor(
                weight[:], shares[h][:, within_half], centre[:], leaned[h][:, within_half], ALU.mult, ALU.subtract
            )
            nc.scalar.activation(out=gated[:], in_=weight[:], func=ACT.Tanh, scale=gate[:])
            nc.vector.tensor_tensor(result[:], gated[:], base_sb[:, cols], ALU.add)
            nc.sync.dma_start(out=out[:, cols], in_=result[:])
